import numpy as np
import ml_dtypes


def mxq(x, axis, fmt="e4m3"):
    dtype, down = {"e4m3": (ml_dtypes.float8_e4m3fn, 7), "e5m2": (ml_dtypes.float8_e5m2, 14)}[fmt]
    v = np.moveaxis(np.asarray(x, np.float32).astype(ml_dtypes.bfloat16).astype(np.float64), axis, -1)
    blocks = v.reshape(v.shape[:-1] + (-1, 32))
    amax = np.abs(blocks).max(-1, keepdims=True)
    byte = np.maximum(np.where(amax > 0, np.frexp(amax)[1] - 1 + 127, 0) - down, 1)
    scale = np.exp2(byte - 127.0)
    codes = (blocks / scale).astype(np.float32).astype(dtype).astype(np.float64)
    return np.moveaxis((codes * scale).reshape(v.shape), -1, axis)


WIDE = False


def mx_kscale(k):
    if not WIDE:
        return np.ones(k)
    levels = np.array([10, -10, 5, -5, 0])
    if k % 512:
        return np.exp2(np.random.permutation(np.resize(levels, k // 32))).repeat(32)
    a = np.empty((k // 512, 16))
    for p in range(k // 512):
        a[p, :8] = np.random.permutation(np.resize(levels, 8))
        for g in range(8):
            far = levels[np.abs(levels - a[p, g]) >= 10]
            a[p, g + 8] = far[np.random.randint(len(far))]
    return np.exp2(a.ravel()).repeat(32)


def f64(x):
    return np.asarray(x).astype(np.float64)


def striped(idx):
    return np.tile(idx.reshape(-1, 16).T, (8, 1)).astype(np.uint16)


def unstriped(offs):
    return offs[:16].T.reshape(-1).astype(np.int64)


def striped8(idx):
    return np.concatenate([x.reshape(-1, 16).T for x in idx]).astype(np.uint16)


def runs(offs, k):
    lists = np.stack([offs[16 * r : 16 * r + 16].T.reshape(-1) for r in range(8)]).astype(np.int64)
    return lists[np.arange(k) % 512 // 64]


def pack_weight(w):
    k, n = w.shape
    w = f64(np.asarray(w, np.float32).astype(ml_dtypes.bfloat16)).reshape(k // 32, 32, n)
    amax = np.abs(w).max(1)
    byte = np.clip(np.where(amax > 0, np.frexp(amax)[1] - 1 + 127 - 7, 1), 1, 254)
    scaled = (w * np.exp2(127.0 - byte)[:, None, :]).reshape(k, n).astype(np.float32)
    words = np.ascontiguousarray(scaled.reshape(k // 512, 128, 4, n).transpose(0, 1, 3, 2)).astype(ml_dtypes.float8_e4m3fn).view(np.uint8)
    return words, np.ascontiguousarray(byte.astype(np.uint8).reshape(k // 512, 16, n))


def unpack_weight(words, scales):
    g, p, n, _ = words.shape
    vals = np.ascontiguousarray(words).view(ml_dtypes.float8_e4m3fn).astype(np.float64) * np.repeat(np.exp2(scales.astype(np.float64) - 127.0), 8, axis=1)[..., None]
    return vals.transpose(0, 1, 3, 2).reshape(g * 512, n)


def sigmoid(v):
    return 1.0 / (1.0 + np.exp(-np.maximum(v, -700.0)))

def planes(y):
    n, m = y.shape
    v = y.astype(np.float32).astype(ml_dtypes.bfloat16).astype(np.float64).reshape(n // 32, 32, m)
    top = np.abs(v).max(1)
    byte = np.clip(np.where(top > 0, np.frexp(top)[1] - 1 + 127 - 7, 1), 1, 254)
    codes = (v * np.exp2(127.0 - byte)[:, None, :]).reshape(n, m).astype(np.float32).astype(ml_dtypes.float8_e4m3fn).view(np.uint8)
    words = codes.reshape(n // 512, 128, 4, m).transpose(0, 1, 3, 2)
    return np.ascontiguousarray(words), np.ascontiguousarray(byte.astype(np.uint8).reshape(n // 512, 16, m))


K, T, S, H, U, C = 512, 2048, 512, 512, 1024, 512


def setup_inputs():
    n = np.random.standard_normal
    s = mx_kscale(K)[:, None]
    packed_xT = pack_weight(n((K, T)) * s)
    packed_w1 = pack_weight(n((K, H)) / np.sqrt(K) / s)
    return {
        "x_words": packed_xT[0],
        "x_scales": packed_xT[1],
        "w1_words": packed_w1[0],
        "w1_scales": packed_w1[1],
        "mem": n((H, U)).astype(np.float32),
        "gs": (np.random.uniform(0.5, 1.5, (K, 1)) / s).astype(np.float32),
        "offs": striped(np.random.permutation(T)[:S]),
        "n1": striped8(np.stack([np.random.permutation(U)[:S] for _ in range(8)])),
        "cand": striped(np.random.permutation(T)[:C]),
        "n2": striped8(np.stack([np.random.permutation(U) for _ in range(8)])),
        "n3": striped8(np.stack([np.random.permutation(U) for _ in range(8)])),
    }


def reference(x_words, x_scales, w1_words, w1_scales, mem, gs, offs, n1, cand, n2, n3):
    x_cand = unpack_weight(x_words, x_scales)[:, unstriped(cand)]
    old = f64(mem)[np.arange(H)[:, None], runs(n1, H)]
    xq = unpack_weight(x_words, x_scales)[:, unstriped(offs)]
    y = unpack_weight(w1_words, w1_scales).T @ xq
    nw = old + sigmoid(y) * (y - old)
    pg = f64(mem).copy()
    pg[np.arange(H)[:, None], runs(n1, H)] = nw
    z = f64(gs) * pg
    s = 0.0625 * ((x_cand.T @ mxq(z, 0, "e4m3")))
    out_0 = (s[np.arange(C)[:, None], runs(n2, C)]) / (np.abs(s) + np.abs(s[np.arange(C)[:, None], runs(n3, C)]) + 0.5)
    return (out_0,) + planes(out_0)

@@ -1,0 +1,235 @@
+from contextlib import ExitStack
+
+import concourse.mybir as mybir
+
+K, T, S, H, U, C = 512, 2048, 512, 512, 1024, 512
+FLOPS = 2 * K * H * S + 2 * K * C * U
+
+F32 = mybir.dt.float32
+BF16 = mybir.dt.bfloat16
+I32 = mybir.dt.int32
+U32 = mybir.dt.uint32
+U16 = mybir.dt.uint16
+U8 = mybir.dt.uint8
+FP8X4 = mybir.dt.float8_e4m3fn_x4
+ACT = mybir.ActivationFunctionType
+ALU = mybir.AluOpType
+
+P = 128
+PACK = 4
+HALF = 512
+
+
+def tile_picked_candpagetnorm2_none_po_kernel(
+    tc, x_words, x_scales, w1_words, w1_scales, mem, gs, offs, n1, cand, n2, n3, out_0, out_1, out_2
+):
+    nc = tc.nc
+    with ExitStack() as ctx:
+        keep = ctx.enter_context(tc.tile_pool(name="keep", bufs=1))
+        ring = ctx.enter_context(tc.tile_pool(name="ring", bufs=2))
+        psum = ctx.enter_context(tc.psum_pool(name="psum", bufs=8))
+
+        def sbuf(name, shape, dtype):
+            return keep.tile(shape, dtype, name=name, align_bytes=64)
+
+        def load_list(name, src):
+            tile = keep.tile(list(src.shape), U16, name=name)
+            nc.sync.dma_start(tile[:], src)
+            return tile
+
+        def load_scale_rows(queue, tile, src):
+            for q in range(4):
+                queue.dma_start(tile[32 * q : 32 * q + 4, :].bitcast(I32), src[0, 4 * q : 4 * q + 4, :].bitcast(I32))
+
+        def words_of(src):
+            return src[0].rearrange("p n t -> p (n t)").bitcast(I32)
+
+        def deal(dst, src):
+            nc.vector.tensor_copy(
+                dst.rearrange("p (t m) -> p m t", t=PACK), src.rearrange("p (m t) -> p m t", t=PACK)
+            )
+
+        xs = sbuf("xs", [P, T], U8)
+        ws = sbuf("ws", [P, H], U8)
+        half = sbuf("half", [P, 1], F32)
+        warm = sbuf("warm", [P, 2], F32)
+        nc.vector.memset(xs[:].bitcast(I32), 0)
+        nc.vector.memset(ws[:].bitcast(I32), 0)
+        nc.vector.memset(half[:], 0.5)
+        nc.scalar.activation(warm[:, 0:1], half[:], ACT.Sigmoid)
+
+        offs_sb = load_list("offs_sb", offs)
+        cand_sb = load_list("cand_sb", cand)
+        ww = sbuf("ww", [P, H], I32)
+        nc.sync.dma_start(ww[:], words_of(w1_words))
+        load_scale_rows(nc.sync, xs, x_scales)
+        xw = sbuf("xw", [P, T], U32)
+        nc.sync.dma_start(xw[:].bitcast(I32), words_of(x_words))
+        load_scale_rows(nc.sync, ws, w1_scales)
+        n1_sb = load_list("n1_sb", n1)
+        page = []
+        mem_rows = mem.rearrange("(p t) u -> p t u", t=PACK)
+        for t in range(PACK):
+            page.append(sbuf("page%d" % t, [P, U], F32))
+            nc.sync.dma_start(page[t][:], mem_rows[:, t, :])
+        gs_sb = sbuf("gs_sb", [P, PACK], F32)
+        nc.sync.dma_start(gs_sb[:], gs.rearrange("(p t) o -> p (t o)", t=PACK))
+        n3_sb = load_list("n3_sb", n3)
+        n2_sb = load_list("n2_sb", n2)
+
+        tok_s = sbuf("tok_s", [P, S], U8)
+        tok_w = sbuf("tok_w", [P, S], U32)
+        cand_s = sbuf("cand_s", [P, C], U8)
+        cand_w = sbuf("cand_w", [P, C], U32)
+        ws_d = sbuf("ws_d", [P, H], U8)
+        ww_d = sbuf("ww_d", [P, H], I32)
+        cand_sd = sbuf("cand_sd", [P, C], U8)
+        cand_wd = sbuf("cand_wd", [P, C], I32)
+        nc.vector.tensor_copy(tok_s[:], xs[:].indirect(offs_sb[:]))
+        deal(ww_d[:], ww[:])
+        nc.vector.tensor_copy(tok_w[:], xw[:].indirect(offs_sb[:]))
+        deal(ws_d[:], ws[:])
+
+        y, keep_w, new_v, kept = [], [], [], []
+        for t in range(PACK):
+            cols = slice(P * t, P * (t + 1))
+            y.append(psum.tile([P, S], F32, name="y%d" % t, tag="bank"))
+            nc.tensor.matmul_mx(
+                out=y[t][:],
+                lhsT=ww_d[:, cols].bitcast(FP8X4),
+                lhsT_scale=ws_d[:, cols],
+                rhs=tok_w[:].bitcast(FP8X4),
+                rhs_scale=tok_s[:],
+                start=True,
+                stop=True,
+            )
+            keep_w.append(sbuf("keep_w%d" % t, [P, S], F32))
+            new_v.append(sbuf("new_v%d" % t, [P, S], F32))
+            kept.append(sbuf("kept%d" % t, [P, S], F32))
+            nc.scalar.activation(keep_w[t][:], y[t][:], ACT.Sigmoid, scale=-1.0)
+        for t in range(PACK):
+            nc.scalar.activation(new_v[t][:], y[t][:], ACT.Silu)
+        nc.scalar.activation(
+            warm[:, 1:2], new_v[PACK - 1][:, 0:1], ACT.Abs_reciprocal_sqrt, scale=keep_w[PACK - 1][:, 0:1], bias=half[:]
+        )
+
+        nc.vector.tensor_copy(cand_s[:], xs[:].indirect(cand_sb[:]))
+        nc.vector.tensor_copy(cand_w[:], xw[:].indirect(cand_sb[:]))
+        deal(cand_sd[:], cand_s[:])
+        deal(cand_wd[:], cand_w[:].bitcast(I32))
+
+        z_woven = [sbuf("z_woven%d" % h, [P, HALF, PACK], BF16) for h in range(2)]
+        z_rows = sbuf("z_rows", [P, PACK, HALF], BF16)
+
+        def fetch_old(t):
+            nc.vector.tensor_tensor(kept[t][:], page[t][:].indirect(n1_sb[:]), keep_w[t][:], ALU.mult)
+
+        def put_new(t):
+            nc.vector.tensor_tensor(page[t][:].indirect(n1_sb[:]), kept[t][:], new_v[t][:], ALU.add)
+            g = gs_sb[:, t : t + 1]
+            nc.scalar.activation(z_woven[0][:, :, t], page[t][:, 0:HALF], ACT.Copy, scale=g)
+            if t < PACK - 1:
+                nc.scalar.activation(z_rows[:, t, :], page[t][:, HALF:U], ACT.Copy, scale=g)
+            else:
+                nc.vector.tensor_scalar(z_rows[:, t, :], page[t][:, HALF:U], g, None, ALU.mult)
+
+        for t in range(PACK):
+            fetch_old(t)
+        for t in range(PACK):
+            put_new(t)
+        nc.vector.tensor_copy(z_woven[1][:], z_rows[:].rearrange("p t w -> p w t"))
+        z_w = [sbuf("z_w%d" % h, [P, HALF], U32) for h in range(2)]
+        z_s = [sbuf("z_s%d" % h, [P, HALF], U8) for h in range(2)]
+        for h in range(2):
+            nc.vector.quantize_mx(
+                out=z_w[h][:].bitcast(FP8X4), scales=z_s[h][:], in_=z_woven[h][:].rearrange("p w t -> p (w t)")
+            )
+
+        out_rows = out_0.rearrange("(p t) u -> p t u", t=PACK)
+        res = [sbuf("res%d" % h, [P, PACK, HALF], F32) for h in range(2)]
+        banks = {}
+        for t in range(PACK):
+            cols = slice(P * t, P * (t + 1))
+            for h in range(2):
+                banks[t, h] = psum.tile([P, HALF], F32, name="s%d_%d" % (t, h), tag="bank")
+                nc.tensor.matmul_mx(
+                    out=banks[t, h][:],
+                    lhsT=cand_wd[:, cols].bitcast(FP8X4),
+                    lhsT_scale=cand_sd[:, cols],
+                    rhs=z_w[h][:].bitcast(FP8X4),
+                    rhs_scale=z_s[h][:],
+                    start=True,
+                    stop=True,
+                )
+        score = [sbuf("score%d" % t, [P, U], F32) for t in range(PACK)]
+        size = [sbuf("size%d" % t, [P, U], F32) for t in range(PACK)]
+        own = [sbuf("own%d" % t, [P, U], F32) for t in range(PACK)]
+        den = {}
+
+        def span(h):
+            return slice(HALF * h, HALF * (h + 1))
+
+        def entries(h):
+            return slice(32 * h, 32 * (h + 1))
+
+        def sizes(t):
+            for h in range(2):
+                nc.scalar.activation(size[t][:, span(h)], banks[t, h][:], ACT.Abs, scale=0.0625)
+            if t == 0:
+                nc.vector.tensor_copy(own[t][:], size[t][:])
+            else:
+                nc.sync.dma_start(own[t][:], size[t][:])
+            for h in range(2):
+                den[t, h] = sbuf("den%d_%d" % (t, h), [P, HALF], F32)
+                nc.vector.tensor_tensor(
+                    den[t, h][:], size[t][:].indirect(n3_sb[:, entries(h)]), own[t][:, span(h)], ALU.add
+                )
+
+        def scores(t):
+            for h in range(2):
+                if t == 0:
+                    nc.vector.tensor_scalar(score[t][:, span(h)], banks[t, h][:], 0.0625, None, ALU.mult)
+                else:
+                    nc.scalar.activation(score[t][:, span(h)], banks[t, h][:], ACT.Copy, scale=0.0625)
+
+        def finish(t, h):
+            root = ring.tile([P, HALF], F32, name="root")
+            inv = sbuf("inv%d_%d" % (t, h), [P, HALF], F32)
+            nc.scalar.activation(root[:], den[t, h][:], ACT.Abs_reciprocal_sqrt, bias=half[:])
+            nc.scalar.activation(inv[:], root[:], ACT.Square)
+            nc.vector.tensor_tensor(res[h][:, t, :], score[t][:].indirect(n2_sb[:, entries(h)]), inv[:], ALU.mult)
+            nc.sync.dma_start(out_rows[:, t, span(h)], res[h][:, t, :])
+
+        scores(0)
+        sizes(0)
+        sizes(1)
+        sizes(2)
+        finish(0, 0)
+        scores(1)
+        finish(1, 0)
+        sizes(3)
+        scores(2)
+        finish(2, 0)
+        finish(0, 1)
+        scores(3)
+        finish(3, 0)
+        finish(1, 1)
+        finish(2, 1)
+        finish(3, 1)
+
+        out_words = words_of(out_1)
+        res_s = sbuf("res_s", [P, U], U8)
+        woven = [sbuf("woven%d" % h, [P, HALF, PACK], BF16) for h in range(2)]
+        nc.scalar.copy(woven[0][:], res[0][:].rearrange("p t w -> p w t"))
+        nc.vector.tensor_copy(woven[1][:], res[1][:].rearrange("p t w -> p w t"))
+        for h in (1, 0):
+            res_w = sbuf("res_w%d" % h, [P, HALF], U32)
+            nc.vector.quantize_mx(
+                out=res_w[:].bitcast(FP8X4),
+                scales=res_s[:, HALF * h : HALF * (h + 1)],
+                in_=woven[h][:].rearrange("p w t -> p (w t)"),
+            )
+            nc.sync.dma_start(out_words[:, HALF * h : HALF * (h + 1)], res_w[:].bitcast(I32))
+        for q in range(4):
+            queue = nc.sync if q % 2 == 0 else nc.scalar
+            queue.dma_start(out_2[0, 4 * q : 4 * q + 4, :].bitcast(I32), res_s[32 * q : 32 * q + 4, :].bitcast(I32))

@@ -29,17 +29,20 @@ def tile_picked_candpagetnorm2_none_po_kernel(
         ring = ctx.enter_context(tc.tile_pool(name="ring", bufs=2))
         psum = ctx.enter_context(tc.psum_pool(name="psum", bufs=8))
 
-        def sbuf(name, shape, dtype):
-            return keep.tile(shape, dtype, name=name, align_bytes=64)
+        def sbuf(name, shape, dtype, tag=None):
+            return keep.tile(shape, dtype, name=name, tag=tag or name, align_bytes=64)
 
         def load_list(name, src):
             tile = keep.tile(list(src.shape), U16, name=name)
             nc.sync.dma_start(tile[:], src)
             return tile
 
-        def load_scale_rows(queue, tile, src):
+        def load_scale_rows(tile, src):
             for q in range(4):
-                queue.dma_start(tile[32 * q : 32 * q + 4, :].bitcast(I32), src[0, 4 * q : 4 * q + 4, :].bitcast(I32))
+                rows = src[0, 4 * q : 4 * q + 4, :].bitcast(I32)
+                nc.sync.dma_start(
+                    tile[32 * q : 32 * (q + 1), :].bitcast(I32), rows.unsqueeze(0).to_broadcast([8, 4, rows.shape[1]])
+                )
 
         def words_of(src):
             return src[0].rearrange("p n t -> p (n t)").bitcast(I32)
@@ -49,23 +52,24 @@ def tile_picked_candpagetnorm2_none_po_kernel(
                 dst.rearrange("p (t m) -> p m t", t=PACK), src.rearrange("p (m t) -> p m t", t=PACK)
             )
 
+        def weave(engine_copy, dst, src):
+            engine_copy(dst.rearrange("p (c i) t -> p c t i", i=4), src.rearrange("p t (c i) -> p c t i", i=4))
+
         xs = sbuf("xs", [P, T], U8)
         ws = sbuf("ws", [P, H], U8)
         half = sbuf("half", [P, 1], F32)
         warm = sbuf("warm", [P, 2], F32)
-        nc.vector.memset(xs[:].bitcast(I32), 0)
-        nc.vector.memset(ws[:].bitcast(I32), 0)
         nc.vector.memset(half[:], 0.5)
         nc.scalar.activation(warm[:, 0:1], half[:], ACT.Sigmoid)
 
         offs_sb = load_list("offs_sb", offs)
+        load_scale_rows(xs, x_scales)
         cand_sb = load_list("cand_sb", cand)
-        ww = sbuf("ww", [P, H], I32)
-        nc.sync.dma_start(ww[:], words_of(w1_words))
-        load_scale_rows(nc.sync, xs, x_scales)
         xw = sbuf("xw", [P, T], U32)
         nc.sync.dma_start(xw[:].bitcast(I32), words_of(x_words))
-        load_scale_rows(nc.sync, ws, w1_scales)
+        ww = sbuf("ww", [P, H], I32)
+        nc.sync.dma_start(ww[:], words_of(w1_words))
+        load_scale_rows(ws, w1_scales)
         n1_sb = load_list("n1_sb", n1)
         page = []
         mem_rows = mem.rearrange("(p t) u -> p t u", t=PACK)
@@ -80,14 +84,12 @@ def tile_picked_candpagetnorm2_none_po_kernel(
         tok_s = sbuf("tok_s", [P, S], U8)
         tok_w = sbuf("tok_w", [P, S], U32)
         cand_s = sbuf("cand_s", [P, C], U8)
-        cand_w = sbuf("cand_w", [P, C], U32)
         ws_d = sbuf("ws_d", [P, H], U8)
         ww_d = sbuf("ww_d", [P, H], I32)
-        cand_sd = sbuf("cand_sd", [P, C], U8)
         cand_wd = sbuf("cand_wd", [P, C], I32)
         nc.vector.tensor_copy(tok_s[:], xs[:].indirect(offs_sb[:]))
-        deal(ww_d[:], ww[:])
         nc.vector.tensor_copy(tok_w[:], xw[:].indirect(offs_sb[:]))
+        deal(ww_d[:], ww[:])
         deal(ws_d[:], ws[:])
 
         y, keep_w, new_v, kept = [], [], [], []
@@ -114,11 +116,13 @@ def tile_picked_candpagetnorm2_none_po_kernel(
         )
 
         nc.vector.tensor_copy(cand_s[:], xs[:].indirect(cand_sb[:]))
+        cand_w = sbuf("cand_w", [P, C], U32, tag="ws")
         nc.vector.tensor_copy(cand_w[:], xw[:].indirect(cand_sb[:]))
-        deal(cand_sd[:], cand_s[:])
+        cand_sd = sbuf("cand_sd", [P, C], U8, tag="ww")
         deal(cand_wd[:], cand_w[:].bitcast(I32))
+        deal(cand_sd[:], cand_s[:])
 
-        z_woven = [sbuf("z_woven%d" % h, [P, HALF, PACK], BF16) for h in range(2)]
+        z_woven = sbuf("z_woven", [P, U, PACK], BF16)
         z_rows = sbuf("z_rows", [P, PACK, HALF], BF16)
 
         def fetch_old(t):
@@ -127,7 +131,7 @@ def tile_picked_candpagetnorm2_none_po_kernel(
         def put_new(t):
             nc.vector.tensor_tensor(page[t][:].indirect(n1_sb[:]), kept[t][:], new_v[t][:], ALU.add)
             g = gs_sb[:, t : t + 1]
-            nc.scalar.activation(z_woven[0][:, :, t], page[t][:, 0:HALF], ACT.Copy, scale=g)
+            nc.scalar.activation(z_woven[:, 0:HALF, t], page[t][:, 0:HALF], ACT.Copy, scale=g)
             if t < PACK - 1:
                 nc.scalar.activation(z_rows[:, t, :], page[t][:, HALF:U], ACT.Copy, scale=g)
             else:
@@ -137,13 +141,10 @@ def tile_picked_candpagetnorm2_none_po_kernel(
             fetch_old(t)
         for t in range(PACK):
             put_new(t)
-        nc.vector.tensor_copy(z_woven[1][:], z_rows[:].rearrange("p t w -> p w t"))
-        z_w = [sbuf("z_w%d" % h, [P, HALF], U32) for h in range(2)]
-        z_s = [sbuf("z_s%d" % h, [P, HALF], U8) for h in range(2)]
-        for h in range(2):
-            nc.vector.quantize_mx(
-                out=z_w[h][:].bitcast(FP8X4), scales=z_s[h][:], in_=z_woven[h][:].rearrange("p w t -> p (w t)")
-            )
+        weave(nc.vector.tensor_copy, z_woven[:, HALF:U, :], z_rows[:])
+        z_w = sbuf("z_w", [P, U], U32)
+        z_s = sbuf("z_s", [P, U], U8)
+        nc.vector.quantize_mx(out=z_w[:].bitcast(FP8X4), scales=z_s[:], in_=z_woven[:].rearrange("p w t -> p (w t)"))
 
         out_rows = out_0.rearrange("(p t) u -> p t u", t=PACK)
         res = [sbuf("res%d" % h, [P, PACK, HALF], F32) for h in range(2)]
@@ -156,8 +157,8 @@ def tile_picked_candpagetnorm2_none_po_kernel(
                     out=banks[t, h][:],
                     lhsT=cand_wd[:, cols].bitcast(FP8X4),
                     lhsT_scale=cand_sd[:, cols],
-                    rhs=z_w[h][:].bitcast(FP8X4),
-                    rhs_scale=z_s[h][:],
+                    rhs=z_w[:, HALF * h : HALF * (h + 1)].bitcast(FP8X4),
+                    rhs_scale=z_s[:, HALF * h : HALF * (h + 1)],
                     start=True,
                     stop=True,
                 )
@@ -175,11 +176,11 @@ def tile_picked_candpagetnorm2_none_po_kernel(
         def sizes(t):
             for h in range(2):
                 nc.scalar.activation(size[t][:, span(h)], banks[t, h][:], ACT.Abs, scale=0.0625)
-            if t == 0:
-                nc.vector.tensor_copy(own[t][:], size[t][:])
-            else:
-                nc.sync.dma_start(own[t][:], size[t][:])
+                if t > 0:
+                    nc.scalar.dma_start(own[t][:, span(h)], size[t][:, span(h)])
             for h in range(2):
+                if t == 0:
+                    nc.vector.tensor_copy(own[t][:, span(h)], size[t][:, span(h)])
                 den[t, h] = sbuf("den%d_%d" % (t, h), [P, HALF], F32)
                 nc.vector.tensor_tensor(
                     den[t, h][:], size[t][:].indirect(n3_sb[:, entries(h)]), own[t][:, span(h)], ALU.add
@@ -187,7 +188,7 @@ def tile_picked_candpagetnorm2_none_po_kernel(
 
         def scores(t):
             for h in range(2):
-                if t == 0:
+                if t == 0 and h == 0:
                     nc.vector.tensor_scalar(score[t][:, span(h)], banks[t, h][:], 0.0625, None, ALU.mult)
                 else:
                     nc.scalar.activation(score[t][:, span(h)], banks[t, h][:], ACT.Copy, scale=0.0625)
@@ -197,14 +198,23 @@ def tile_picked_candpagetnorm2_none_po_kernel(
             inv = sbuf("inv%d_%d" % (t, h), [P, HALF], F32)
             nc.scalar.activation(root[:], den[t, h][:], ACT.Abs_reciprocal_sqrt, bias=half[:])
             nc.scalar.activation(inv[:], root[:], ACT.Square)
-            nc.vector.tensor_tensor(res[h][:, t, :], score[t][:].indirect(n2_sb[:, entries(h)]), inv[:], ALU.mult)
-            nc.sync.dma_start(out_rows[:, t, span(h)], res[h][:, t, :])
+            pieces = 2 if (t, h) == (PACK - 1, 1) else 1
+            width = HALF // pieces
+            for a in range(0, HALF, width):
+                first = HALF * h + a
+                nc.vector.tensor_tensor(
+                    res[h][:, t, a : a + width],
+                    score[t][:].indirect(n2_sb[:, first // 16 : (first + width) // 16]),
+                    inv[:, a : a + width],
+                    ALU.mult,
+                )
+                nc.sync.dma_start(out_rows[:, t, first : first + width], res[h][:, t, a : a + width])
 
-        scores(0)
         sizes(0)
         sizes(1)
-        sizes(2)
+        scores(0)
         finish(0, 0)
+        sizes(2)
         scores(1)
         finish(1, 0)
         sizes(3)
@@ -220,9 +230,10 @@ def tile_picked_candpagetnorm2_none_po_kernel(
         out_words = words_of(out_1)
         res_s = sbuf("res_s", [P, U], U8)
         woven = [sbuf("woven%d" % h, [P, HALF, PACK], BF16) for h in range(2)]
-        nc.scalar.copy(woven[0][:], res[0][:].rearrange("p t w -> p w t"))
-        nc.vector.tensor_copy(woven[1][:], res[1][:].rearrange("p t w -> p w t"))
-        for h in (1, 0):
+        weave(nc.scalar.copy, woven[0][:], res[0][:])
+        weave(nc.scalar.copy, woven[1][:, 0 : HALF // 2, :], res[1][:, :, 0 : HALF // 2])
+        weave(nc.vector.tensor_copy, woven[1][:, HALF // 2 : HALF, :], res[1][:, :, HALF // 2 : HALF])
+        for h in range(2):
             res_w = sbuf("res_w%d" % h, [P, HALF], U32)
             nc.vector.quantize_mx(
                 out=res_w[:].bitcast(FP8X4),

@@ -18,6 +18,7 @@ ALU = mybir.AluOpType
 P = 128
 PACK = 4
 HALF = 512
+SPLIT = 208
 
 
 def tile_picked_candpagetnorm2_none_po_kernel(
@@ -119,11 +120,11 @@ def tile_picked_candpagetnorm2_none_po_kernel(
         cand_w = sbuf("cand_w", [P, C], U32, tag="ws")
         nc.vector.tensor_copy(cand_w[:], xw[:].indirect(cand_sb[:]))
         cand_sd = sbuf("cand_sd", [P, C], U8, tag="ww")
-        deal(cand_wd[:], cand_w[:].bitcast(I32))
         deal(cand_sd[:], cand_s[:])
+        deal(cand_wd[:], cand_w[:].bitcast(I32))
 
-        z_woven = sbuf("z_woven", [P, U, PACK], BF16)
-        z_rows = sbuf("z_rows", [P, PACK, HALF], BF16)
+        z_woven = sbuf("z_woven", [P, 2, HALF, PACK], BF16)
+        z_pair = sbuf("z_pair", [P, 2, 2, HALF - SPLIT], BF16)
 
         def fetch_old(t):
             nc.vector.tensor_tensor(kept[t][:], page[t][:].indirect(n1_sb[:]), keep_w[t][:], ALU.mult)
@@ -131,20 +132,32 @@ def tile_picked_candpagetnorm2_none_po_kernel(
         def put_new(t):
             nc.vector.tensor_tensor(page[t][:].indirect(n1_sb[:]), kept[t][:], new_v[t][:], ALU.add)
             g = gs_sb[:, t : t + 1]
-            nc.scalar.activation(z_woven[:, 0:HALF, t], page[t][:, 0:HALF], ACT.Copy, scale=g)
-            if t < PACK - 1:
-                nc.scalar.activation(z_rows[:, t, :], page[t][:, HALF:U], ACT.Copy, scale=g)
+            halves = page[t][:].rearrange("p (h w) -> p h w", h=2)
+            if t < 2:
+                nc.scalar.activation(z_woven[:, :, :, t], halves, ACT.Copy, scale=g)
+                return
+            for h in (1, 0):
+                nc.scalar.activation(z_woven[:, h, 0:SPLIT, t], halves[:, h, 0:SPLIT], ACT.Copy, scale=g)
+            if t == 2:
+                nc.scalar.activation(z_pair[:, 0, :, :], halves[:, :, SPLIT:HALF], ACT.Copy, scale=g)
             else:
-                nc.vector.tensor_scalar(z_rows[:, t, :], page[t][:, HALF:U], g, None, ALU.mult)
+                nc.vector.tensor_scalar(z_pair[:, 1, :, :], halves[:, :, SPLIT:HALF], g, None, ALU.mult)
 
         for t in range(PACK):
             fetch_old(t)
         for t in range(PACK):
             put_new(t)
-        weave(nc.vector.tensor_copy, z_woven[:, HALF:U, :], z_rows[:])
+        for h in range(2):
+            nc.vector.tensor_copy(z_woven[:, h, SPLIT:HALF, 2:4], z_pair[:, :, h, :].rearrange("p t w -> p w t"))
         z_w = sbuf("z_w", [P, U], U32)
         z_s = sbuf("z_s", [P, U], U8)
-        nc.vector.quantize_mx(out=z_w[:].bitcast(FP8X4), scales=z_s[:], in_=z_woven[:].rearrange("p w t -> p (w t)"))
+        for h in range(2):
+            cols = slice(HALF * h, HALF * (h + 1))
+            nc.vector.quantize_mx(
+                out=z_w[:, cols].bitcast(FP8X4),
+                scales=z_s[:, cols],
+                in_=z_woven[:, h, :, :].rearrange("p w t -> p (w t)"),
+            )
 
         out_rows = out_0.rearrange("(p t) u -> p t u", t=PACK)
         res = [sbuf("res%d" % h, [P, PACK, HALF], F32) for h in range(2)]
@@ -177,21 +190,21 @@ def tile_picked_candpagetnorm2_none_po_kernel(
             for h in range(2):
                 nc.scalar.activation(size[t][:, span(h)], banks[t, h][:], ACT.Abs, scale=0.0625)
                 if t > 0:
-                    nc.scalar.dma_start(own[t][:, span(h)], size[t][:, span(h)])
-            for h in range(2):
-                if t == 0:
+                    nc.sync.dma_start(own[t][:, span(h)], size[t][:, span(h)])
+                else:
                     nc.vector.tensor_copy(own[t][:, span(h)], size[t][:, span(h)])
+            for h in range(2):
                 den[t, h] = sbuf("den%d_%d" % (t, h), [P, HALF], F32)
                 nc.vector.tensor_tensor(
                     den[t, h][:], size[t][:].indirect(n3_sb[:, entries(h)]), own[t][:, span(h)], ALU.add
                 )
 
         def scores(t):
-            for h in range(2):
-                if t == 0 and h == 0:
-                    nc.vector.tensor_scalar(score[t][:, span(h)], banks[t, h][:], 0.0625, None, ALU.mult)
-                else:
-                    nc.scalar.activation(score[t][:, span(h)], banks[t, h][:], ACT.Copy, scale=0.0625)
+            for h in range(1 if t < 2 else 0, 2):
+                nc.scalar.activation(score[t][:, span(h)], banks[t, h][:], ACT.Copy, scale=0.0625)
+
+        def early_score(t):
+            nc.vector.tensor_scalar(score[t][:, span(0)], banks[t, 0][:], 0.0625, None, ALU.mult)
 
         def finish(t, h):
             root = ring.tile([P, HALF], F32, name="root")
@@ -210,17 +223,19 @@ def tile_picked_candpagetnorm2_none_po_kernel(
                 )
                 nc.sync.dma_start(out_rows[:, t, first : first + width], res[h][:, t, a : a + width])
 
+        early_score(1)
         sizes(0)
         sizes(1)
+        early_score(0)
         scores(0)
-        finish(0, 0)
         sizes(2)
+        finish(0, 0)
         scores(1)
-        finish(1, 0)
         sizes(3)
+        finish(1, 0)
         scores(2)
-        finish(2, 0)
         finish(0, 1)
+        finish(2, 0)
         scores(3)
         finish(3, 0)
         finish(1, 1)

@@ -191,8 +191,10 @@ def tile_picked_candpagetnorm2_none_po_kernel(
                 nc.scalar.activation(size[t][:, span(h)], banks[t, h][:], ACT.Abs, scale=0.0625)
                 if t > 0:
                     nc.sync.dma_start(own[t][:, span(h)], size[t][:, span(h)])
-                else:
+                elif h == 0:
                     nc.vector.tensor_copy(own[t][:, span(h)], size[t][:, span(h)])
+                else:
+                    nc.scalar.activation(own[t][:, span(h)], banks[t, h][:], ACT.Abs, scale=0.0625)
             for h in range(2):
                 den[t, h] = sbuf("den%d_%d" % (t, h), [P, HALF], F32)
                 nc.vector.tensor_tensor(
@@ -200,7 +202,7 @@ def tile_picked_candpagetnorm2_none_po_kernel(
                 )
 
         def scores(t):
-            for h in range(1 if t < 2 else 0, 2):
+            for h in range(1 if t == 0 else 0, 2):
                 nc.scalar.activation(score[t][:, span(h)], banks[t, h][:], ACT.Copy, scale=0.0625)
 
         def early_score(t):
@@ -211,9 +213,8 @@ def tile_picked_candpagetnorm2_none_po_kernel(
             inv = sbuf("inv%d_%d" % (t, h), [P, HALF], F32)
             nc.scalar.activation(root[:], den[t, h][:], ACT.Abs_reciprocal_sqrt, bias=half[:])
             nc.scalar.activation(inv[:], root[:], ACT.Square)
-            pieces = 2 if (t, h) == (PACK - 1, 1) else 1
-            width = HALF // pieces
-            for a in range(0, HALF, width):
+            pieces = ((0, 256), (256, 128), (384, 128)) if (t, h) == (PACK - 1, 1) else ((0, HALF),)
+            for a, width in pieces:
                 first = HALF * h + a
                 nc.vector.tensor_tensor(
                     res[h][:, t, a : a + width],
@@ -223,7 +224,6 @@ def tile_picked_candpagetnorm2_none_po_kernel(
                 )
                 nc.sync.dma_start(out_rows[:, t, first : first + width], res[h][:, t, a : a + width])
 
-        early_score(1)
         sizes(0)
         sizes(1)
         early_score(0)
@@ -246,8 +246,9 @@ def tile_picked_candpagetnorm2_none_po_kernel(
         res_s = sbuf("res_s", [P, U], U8)
         woven = [sbuf("woven%d" % h, [P, HALF, PACK], BF16) for h in range(2)]
         weave(nc.scalar.copy, woven[0][:], res[0][:])
-        weave(nc.scalar.copy, woven[1][:, 0 : HALF // 2, :], res[1][:, :, 0 : HALF // 2])
-        weave(nc.vector.tensor_copy, woven[1][:, HALF // 2 : HALF, :], res[1][:, :, HALF // 2 : HALF])
+        weave(nc.scalar.copy, woven[1][:, 0:256, :], res[1][:, :, 0:256])
+        weave(nc.scalar.copy, woven[1][:, 256:384, :], res[1][:, :, 256:384])
+        weave(nc.vector.tensor_copy, woven[1][:, 384:HALF, :], res[1][:, :, 384:HALF])
         for h in range(2):
             res_w = sbuf("res_w%d" % h, [P, HALF], U32)
             nc.vector.quantize_mx(

from contextlib import ExitStack

import concourse.mybir as mybir

K, T, S, H, U, C = 512, 2048, 512, 512, 1024, 512
FLOPS = 2 * K * H * S + 2 * K * C * U

F32 = mybir.dt.float32
BF16 = mybir.dt.bfloat16
I32 = mybir.dt.int32
U32 = mybir.dt.uint32
U16 = mybir.dt.uint16
U8 = mybir.dt.uint8
FP8X4 = mybir.dt.float8_e4m3fn_x4
ACT = mybir.ActivationFunctionType
ALU = mybir.AluOpType

P = 128
PACK = 4
HALF = 512
SPLIT = 208


def tile_picked_candpagetnorm2_none_po_kernel(
    tc, x_words, x_scales, w1_words, w1_scales, mem, gs, offs, n1, cand, n2, n3, out_0, out_1, out_2
):
    nc = tc.nc
    with ExitStack() as ctx:
        keep = ctx.enter_context(tc.tile_pool(name="keep", bufs=1))
        ring = ctx.enter_context(tc.tile_pool(name="ring", bufs=2))
        psum = ctx.enter_context(tc.psum_pool(name="psum", bufs=8))

        def sbuf(name, shape, dtype, tag=None):
            return keep.tile(shape, dtype, name=name, tag=tag or name, align_bytes=64)

        def load_list(name, src):
            tile = keep.tile(list(src.shape), U16, name=name)
            nc.sync.dma_start(tile[:], src)
            return tile

        def load_scale_rows(tile, src):
            for q in range(4):
                rows = src[0, 4 * q : 4 * q + 4, :].bitcast(I32)
                nc.sync.dma_start(
                    tile[32 * q : 32 * (q + 1), :].bitcast(I32), rows.unsqueeze(0).to_broadcast([8, 4, rows.shape[1]])
                )

        def words_of(src):
            return src[0].rearrange("p n t -> p (n t)").bitcast(I32)

        def deal(dst, src):
            nc.vector.tensor_copy(
                dst.rearrange("p (t m) -> p m t", t=PACK), src.rearrange("p (m t) -> p m t", t=PACK)
            )

        def weave(engine_copy, dst, src):
            engine_copy(dst.rearrange("p (c i) t -> p c t i", i=4), src.rearrange("p t (c i) -> p c t i", i=4))

        xs = sbuf("xs", [P, T], U8)
        ws = sbuf("ws", [P, H], U8)
        half = sbuf("half", [P, 1], F32)
        warm = sbuf("warm", [P, 2], F32)
        nc.vector.memset(half[:], 0.5)
        nc.scalar.activation(warm[:, 0:1], half[:], ACT.Sigmoid)

        offs_sb = load_list("offs_sb", offs)
        load_scale_rows(xs, x_scales)
        cand_sb = load_list("cand_sb", cand)
        xw = sbuf("xw", [P, T], U32)
        nc.sync.dma_start(xw[:].bitcast(I32), words_of(x_words))
        ww = sbuf("ww", [P, H], I32)
        nc.sync.dma_start(ww[:], words_of(w1_words))
        load_scale_rows(ws, w1_scales)
        n1_sb = load_list("n1_sb", n1)
        page = []
        mem_rows = mem.rearrange("(p t) u -> p t u", t=PACK)
        for t in range(PACK):
            page.append(sbuf("page%d" % t, [P, U], F32))
            nc.sync.dma_start(page[t][:], mem_rows[:, t, :])
        gs_sb = sbuf("gs_sb", [P, PACK], F32)
        nc.sync.dma_start(gs_sb[:], gs.rearrange("(p t) o -> p (t o)", t=PACK))
        n3_sb = load_list("n3_sb", n3)
        n2_sb = load_list("n2_sb", n2)

        tok_s = sbuf("tok_s", [P, S], U8)
        tok_w = sbuf("tok_w", [P, S], U32)
        cand_s = sbuf("cand_s", [P, C], U8)
        ws_d = sbuf("ws_d", [P, H], U8)
        ww_d = sbuf("ww_d", [P, H], I32)
        cand_wd = sbuf("cand_wd", [P, C], I32)
        nc.vector.tensor_copy(tok_s[:], xs[:].indirect(offs_sb[:]))
        nc.vector.tensor_copy(tok_w[:], xw[:].indirect(offs_sb[:]))
        deal(ww_d[:], ww[:])
        deal(ws_d[:], ws[:])

        y, keep_w, new_v, kept = [], [], [], []
        for t in range(PACK):
            cols = slice(P * t, P * (t + 1))
            y.append(psum.tile([P, S], F32, name="y%d" % t, tag="bank"))
            nc.tensor.matmul_mx(
                out=y[t][:],
                lhsT=ww_d[:, cols].bitcast(FP8X4),
                lhsT_scale=ws_d[:, cols],
                rhs=tok_w[:].bitcast(FP8X4),
                rhs_scale=tok_s[:],
                start=True,
                stop=True,
            )
            keep_w.append(sbuf("keep_w%d" % t, [P, S], F32))
            new_v.append(sbuf("new_v%d" % t, [P, S], F32))
            kept.append(sbuf("kept%d" % t, [P, S], F32))
            nc.scalar.activation(keep_w[t][:], y[t][:], ACT.Sigmoid, scale=-1.0)
        for t in range(PACK):
            nc.scalar.activation(new_v[t][:], y[t][:], ACT.Silu)
        nc.scalar.activation(
            warm[:, 1:2], new_v[PACK - 1][:, 0:1], ACT.Abs_reciprocal_sqrt, scale=keep_w[PACK - 1][:, 0:1], bias=half[:]
        )

        nc.vector.tensor_copy(cand_s[:], xs[:].indirect(cand_sb[:]))
        cand_w = sbuf("cand_w", [P, C], U32, tag="ws")
        nc.vector.tensor_copy(cand_w[:], xw[:].indirect(cand_sb[:]))
        cand_sd = sbuf("cand_sd", [P, C], U8, tag="ww")
        deal(cand_sd[:], cand_s[:])
        deal(cand_wd[:], cand_w[:].bitcast(I32))

        z_woven = sbuf("z_woven", [P, 2, HALF, PACK], BF16)
        z_pair = sbuf("z_pair", [P, 2, 2, HALF - SPLIT], BF16)

        def fetch_old(t):
            nc.vector.tensor_tensor(kept[t][:], page[t][:].indirect(n1_sb[:]), keep_w[t][:], ALU.mult)

        def put_new(t):
            nc.vector.tensor_tensor(page[t][:].indirect(n1_sb[:]), kept[t][:], new_v[t][:], ALU.add)
            g = gs_sb[:, t : t + 1]
            halves = page[t][:].rearrange("p (h w) -> p h w", h=2)
            if t < 2:
                nc.scalar.activation(z_woven[:, :, :, t], halves, ACT.Copy, scale=g)
                return
            for h in (1, 0):
                nc.scalar.activation(z_woven[:, h, 0:SPLIT, t], halves[:, h, 0:SPLIT], ACT.Copy, scale=g)
            if t == 2:
                nc.scalar.activation(z_pair[:, 0, :, :], halves[:, :, SPLIT:HALF], ACT.Copy, scale=g)
            else:
                nc.vector.tensor_scalar(z_pair[:, 1, :, :], halves[:, :, SPLIT:HALF], g, None, ALU.mult)

        for t in range(PACK):
            fetch_old(t)
        for t in range(PACK):
            put_new(t)
        for h in range(2):
            nc.vector.tensor_copy(z_woven[:, h, SPLIT:HALF, 2:4], z_pair[:, :, h, :].rearrange("p t w -> p w t"))
        z_w = sbuf("z_w", [P, U], U32)
        z_s = sbuf("z_s", [P, U], U8)
        for h in range(2):
            cols = slice(HALF * h, HALF * (h + 1))
            nc.vector.quantize_mx(
                out=z_w[:, cols].bitcast(FP8X4),
                scales=z_s[:, cols],
                in_=z_woven[:, h, :, :].rearrange("p w t -> p (w t)"),
            )

        out_rows = out_0.rearrange("(p t) u -> p t u", t=PACK)
        res = [sbuf("res%d" % h, [P, PACK, HALF], F32) for h in range(2)]
        banks = {}
        for t in range(PACK):
            cols = slice(P * t, P * (t + 1))
            for h in range(2):
                banks[t, h] = psum.tile([P, HALF], F32, name="s%d_%d" % (t, h), tag="bank")
                nc.tensor.matmul_mx(
                    out=banks[t, h][:],
                    lhsT=cand_wd[:, cols].bitcast(FP8X4),
                    lhsT_scale=cand_sd[:, cols],
                    rhs=z_w[:, HALF * h : HALF * (h + 1)].bitcast(FP8X4),
                    rhs_scale=z_s[:, HALF * h : HALF * (h + 1)],
                    start=True,
                    stop=True,
                )
        score = [sbuf("score%d" % t, [P, U], F32) for t in range(PACK)]
        size = [sbuf("size%d" % t, [P, U], F32) for t in range(PACK)]
        own = [sbuf("own%d" % t, [P, U], F32) for t in range(PACK)]
        den = {}

        def span(h):
            return slice(HALF * h, HALF * (h + 1))

        def entries(h):
            return slice(32 * h, 32 * (h + 1))

        def sizes(t):
            for h in range(2):
                nc.scalar.activation(size[t][:, span(h)], banks[t, h][:], ACT.Abs, scale=0.0625)
                if t > 0:
                    nc.sync.dma_start(own[t][:, span(h)], size[t][:, span(h)])
                elif h == 0:
                    nc.vector.tensor_copy(own[t][:, span(h)], size[t][:, span(h)])
                else:
                    nc.scalar.activation(own[t][:, span(h)], banks[t, h][:], ACT.Abs, scale=0.0625)
            for h in range(2):
                den[t, h] = sbuf("den%d_%d" % (t, h), [P, HALF], F32)
                nc.vector.tensor_tensor(
                    den[t, h][:], size[t][:].indirect(n3_sb[:, entries(h)]), own[t][:, span(h)], ALU.add
                )

        def scores(t):
            for h in range(1 if t == 0 else 0, 2):
                nc.scalar.activation(score[t][:, span(h)], banks[t, h][:], ACT.Copy, scale=0.0625)

        def early_score(t):
            nc.vector.tensor_scalar(score[t][:, span(0)], banks[t, 0][:], 0.0625, None, ALU.mult)

        def finish(t, h):
            root = ring.tile([P, HALF], F32, name="root")
            inv = sbuf("inv%d_%d" % (t, h), [P, HALF], F32)
            nc.scalar.activation(root[:], den[t, h][:], ACT.Abs_reciprocal_sqrt, bias=half[:])
            nc.scalar.activation(inv[:], root[:], ACT.Square)
            pieces = ((0, 256), (256, 128), (384, 128)) if (t, h) == (PACK - 1, 1) else ((0, HALF),)
            for a, width in pieces:
                first = HALF * h + a
                nc.vector.tensor_tensor(
                    res[h][:, t, a : a + width],
                    score[t][:].indirect(n2_sb[:, first // 16 : (first + width) // 16]),
                    inv[:, a : a + width],
                    ALU.mult,
                )
                nc.sync.dma_start(out_rows[:, t, first : first + width], res[h][:, t, a : a + width])

        sizes(0)
        sizes(1)
        early_score(0)
        scores(0)
        sizes(2)
        finish(0, 0)
        scores(1)
        sizes(3)
        finish(1, 0)
        scores(2)
        finish(0, 1)
        finish(2, 0)
        scores(3)
        finish(3, 0)
        finish(1, 1)
        finish(2, 1)
        finish(3, 1)

        out_words = words_of(out_1)
        res_s = sbuf("res_s", [P, U], U8)
        woven = [sbuf("woven%d" % h, [P, HALF, PACK], BF16) for h in range(2)]
        weave(nc.scalar.copy, woven[0][:], res[0][:])
        weave(nc.scalar.copy, woven[1][:, 0:256, :], res[1][:, :, 0:256])
        weave(nc.scalar.copy, woven[1][:, 256:384, :], res[1][:, :, 256:384])
        weave(nc.vector.tensor_copy, woven[1][:, 384:HALF, :], res[1][:, :, 384:HALF])
        for h in range(2):
            res_w = sbuf("res_w%d" % h, [P, HALF], U32)
            nc.vector.quantize_mx(
                out=res_w[:].bitcast(FP8X4),
                scales=res_s[:, HALF * h : HALF * (h + 1)],
                in_=woven[h][:].rearrange("p w t -> p (w t)"),
            )
            nc.sync.dma_start(out_words[:, HALF * h : HALF * (h + 1)], res_w[:].bitcast(I32))
        for q in range(4):
            queue = nc.sync if q % 2 == 0 else nc.scalar
            queue.dma_start(out_2[0, 4 * q : 4 * q + 4, :].bitcast(I32), res_s[32 * q : 32 * q + 4, :].bitcast(I32))
